import numpy as np
import ml_dtypes


def mxq(x, axis, fmt="e4m3"):
    dtype, down = {"e4m3": (ml_dtypes.float8_e4m3fn, 7), "e5m2": (ml_dtypes.float8_e5m2, 14)}[fmt]
    v = np.moveaxis(np.asarray(x, np.float32).astype(ml_dtypes.bfloat16).astype(np.float64), axis, -1)
    blocks = v.reshape(v.shape[:-1] + (-1, 32))
    amax = np.abs(blocks).max(-1, keepdims=True)
    byte = np.maximum(np.where(amax > 0, np.frexp(amax)[1] - 1 + 127, 0) - down, 1)
    scale = np.exp2(byte - 127.0)
    codes = (blocks / scale).astype(np.float32).astype(dtype).astype(np.float64)
    return np.moveaxis((codes * scale).reshape(v.shape), -1, axis)


WIDE = False


def mx_kscale(k):
    if not WIDE:
        return np.ones(k)
    levels = np.array([10, -10, 5, -5, 0])
    if k % 512:
        return np.exp2(np.random.permutation(np.resize(levels, k // 32))).repeat(32)
    a = np.empty((k // 512, 16))
    for p in range(k // 512):
        a[p, :8] = np.random.permutation(np.resize(levels, 8))
        for g in range(8):
            far = levels[np.abs(levels - a[p, g]) >= 10]
            a[p, g + 8] = far[np.random.randint(len(far))]
    return np.exp2(a.ravel()).repeat(32)


def f64(x):
    return np.asarray(x).astype(np.float64)


def striped(idx):
    return np.tile(np.asarray(idx).reshape(-1, 16).T, (8, 1)).astype(np.uint16)


def unstriped(offs):
    return offs[:16].T.reshape(-1).astype(np.int64)


E2M1 = np.array([0.0, 0.5, 1.0, 1.5, 2.0, 3.0, 4.0, 6.0, -0.0, -0.5, -1.0, -1.5, -2.0, -3.0, -4.0, -6.0])


def pack_weight(w, fmt):
    k, n = w.shape
    w = f64(np.asarray(w, np.float32).astype(ml_dtypes.bfloat16)).reshape(k // 32, 32, n)
    amax = np.abs(w).max(1)
    if fmt == "e4m3":
        byte = np.frexp(amax)[1] - 1 + 127 - 7
    else:
        mant, ex = np.frexp(amax / 6.0)
        byte = np.where(mant > 0.5, ex, ex - 1) + 127
    byte = np.clip(np.where(amax > 0, byte, 1), 1, 254)
    scaled = (w * np.exp2(127.0 - byte)[:, None, :]).reshape(k, n).astype(np.float32)
    by_word = np.ascontiguousarray(scaled.reshape(k // 512, 128, 4, n).transpose(0, 1, 3, 2))
    if fmt == "e4m3":
        words = by_word.astype(ml_dtypes.float8_e4m3fn).view(np.uint8)
    else:
        c = by_word.astype(ml_dtypes.float4_e2m1fn).view(np.uint8) & 0xF
        words = (c[..., 0::2] | (c[..., 1::2] << 4)).reshape(k // 512, 128, 2 * n)
    return np.ascontiguousarray(words), np.ascontiguousarray(byte.astype(np.uint8).reshape(k // 512, 16, n))


def unpack_weight(words, scales, fmt):
    g, _, n = scales.shape
    words = np.ascontiguousarray(words).reshape(g, 128, n, -1)
    if fmt == "e4m3":
        vals = words.view(ml_dtypes.float8_e4m3fn).astype(np.float64)
    else:
        nib = np.empty((g, 128, n, 4), np.uint8)
        nib[..., 0::2] = words & 0xF
        nib[..., 1::2] = words >> 4
        vals = E2M1[nib]
    vals = vals * np.repeat(np.exp2(scales.astype(np.float64) - 127.0), 8, axis=1)[..., None]
    return vals.transpose(0, 1, 3, 2).reshape(g * 512, n)


D, T, I, Q, E, U, X = 512, 2048, 512, 128, 512, 1024, 1024


def setup_inputs():
    n = np.random.standard_normal
    idx = np.random.permutation(T)[:I]
    idx2 = np.random.permutation(U)[:I]
    idx3 = np.random.permutation(X)[:I]
    fd = mx_kscale(D)
    fi = mx_kscale(I)
    keysp = pack_weight(n((D, T)) / fd[:, None], "e4m3")
    return {
        "query": (n((D, Q)) * 0.7 / np.sqrt(D) * fd[:, None]).astype(np.float32),
        "query2": (n((D, Q)) * 0.7 / np.sqrt(D) * fd[:, None]).astype(np.float32),
        "keys_words": keysp[0],
        "keys_scales": keysp[1],
        "notes": (n((D, U)) / fd[:, None]).astype(np.float32),
        "os": (np.random.uniform(0.02, 0.08, (1, I)) * fi).astype(np.float32),
        "vals": (n((E, T))).astype(np.float32),
        "vals2": (n((E, X))).astype(np.float32),
        "vsc": (np.random.uniform(0.5, 2.0, (1, I)) / fi).astype(np.float32),
        "offs": striped(idx),
        "offs2": striped(idx2),
        "offs3": striped(idx3),
    }


def reference(query, query2, keys_words, keys_scales, notes, os, vals, vals2, vsc, offs, offs2, offs3):
    idx = unstriped(offs)
    idx2 = unstriped(offs2)
    idx3 = unstriped(offs3)
    keysu = unpack_weight(keys_words, keys_scales, "e4m3")
    queryq = mxq(f64(query), 0, "e4m3")
    keysidxg = keysu[:, idx]
    query2q = mxq(f64(query2), 0, "e4m3")
    notesidx2q = mxq(f64(notes)[:, idx2], 0, "e4m3")
    w = queryq.T @ keysidxg + query2q.T @ notesidx2q
    wo1 = w * f64(os)
    wt1 = wo1.T
    vz = np.maximum(f64(vals)[:, idx], f64(vals2)[:, idx3]) * f64(vsc)
    vt1 = vz.T
    wt1q = mxq(wt1, 0, "e4m3")
    vt1q = mxq(vt1, 0, "e4m3")
    o = wt1q.T @ vt1q
    return o

@@ -1,0 +1,174 @@
+from contextlib import ExitStack
+
+import concourse.mybir as mybir
+from concourse.masks import make_identity
+
+F32 = mybir.dt.float32
+BF16 = mybir.dt.bfloat16
+I32 = mybir.dt.int32
+U32 = mybir.dt.uint32
+U16 = mybir.dt.uint16
+U8 = mybir.dt.uint8
+FP8X4 = mybir.dt.float8_e4m3fn_x4
+COPY = mybir.ActivationFunctionType.Copy
+MULT = mybir.AluOpType.mult
+MAX = mybir.AluOpType.max
+
+P = 128
+PACK = 4
+D, T, SLOTS, Q, E, U, X = 512, 2048, 512, 128, 512, 1024, 1024
+BLOCKS = SLOTS // 32
+RUN = 8
+E_TILES = E // P
+LIST_COLS = SLOTS // 16
+VECTOR_COLS = 20
+
+FLOPS = 2 * Q * SLOTS * D * 2 + 2 * Q * E * SLOTS
+
+
+def dealt(ap):
+    return ap.rearrange("p (t b r) -> p b t r", t=PACK, b=BLOCKS, r=RUN)
+
+
+def listed(ap):
+    return ap.rearrange("p (b t r) -> p b t r", t=PACK, b=BLOCKS, r=RUN)
+
+
+def tile_attend_twosources_mergedvalues_lean_kernel(
+    tc, query, query2, keys_words, keys_scales, notes, osc, vals, vals2, vsc, offs, offs2, offs3, out
+):
+    nc = tc.nc
+    with ExitStack() as ctx:
+        held = ctx.enter_context(tc.tile_pool(name="held", bufs=1))
+        work = ctx.enter_context(tc.tile_pool(name="work", bufs=2))
+        psum = ctx.enter_context(tc.psum_pool(name="psum", bufs=1))
+        psum2 = ctx.enter_context(tc.psum_pool(name="psum2", bufs=2))
+
+        idx = held.tile([P, LIST_COLS], U16, name="idx")
+        idx2 = held.tile([P, LIST_COLS], U16, name="idx2")
+        idx3 = held.tile([P, LIST_COLS], U16, name="idx3")
+        key_words = held.tile([P, T], I32, name="key_words")
+        key_bytes = held.tile([P, T], U8, name="key_bytes")
+        q_raw = [held.tile([P, PACK, Q], F32, name="q_raw%d" % n) for n in range(2)]
+        note_pair = [held.tile([P, 2, U], F32, name="note_pair%d" % h) for h in range(2)]
+        val_a = [held.tile([P, T], F32, name="val_a%d" % c) for c in range(E_TILES)]
+        val_b = [held.tile([P, X], F32, name="val_b%d" % c, tag="val_b%d" % c) for c in range(E_TILES)]
+        factor_rows = held.tile([P, P], F32, name="factor_rows")
+        ident = held.tile([P, P], F32, name="ident")
+
+        nc.gpsimd.memset(key_bytes[:].bitcast(I32), 0)
+        nc.gpsimd.memset(factor_rows[:], 0.0)
+        make_identity(nc, ident[:])
+
+        notes_by_row = notes.rearrange("(p j) u -> p j u", j=PACK)
+        scale_rows = keys_scales[0].bitcast(I32)
+
+        def load_scale_rows(r):
+            nc.sync.dma_start(key_bytes[r:P:32, :].bitcast(I32), scale_rows[r:16:4, :])
+
+        def load_values(c):
+            nc.sync.dma_start(val_a[c][:], vals[c * P : (c + 1) * P, :])
+            if c == 0:
+                for n, vec in enumerate((osc, vsc)):
+                    nc.sync.dma_start(
+                        factor_rows[PACK * n : PACK * (n + 1), :].rearrange("t (b r) -> t b r", r=RUN),
+                        vec[0].rearrange("(b t r) -> t b r", t=PACK, r=RUN),
+                    )
+                nc.sync.dma_start(idx3[:], offs3)
+            nc.sync.dma_start(val_b[c][:], vals2[c * P : (c + 1) * P, :])
+
+        nc.sync.dma_start(key_words[:], keys_words[0].rearrange("p c r -> p (c r)").bitcast(I32))
+        nc.sync.dma_start(idx[:], offs)
+        nc.sync.dma_start(idx2[:], offs2)
+        nc.sync.dma_start(note_pair[0][:], notes_by_row[:, 0:2, :])
+        load_scale_rows(0)
+        load_scale_rows(1)
+        nc.sync.dma_start(note_pair[1][:], notes_by_row[:, 2:4, :])
+        load_scale_rows(2)
+        load_scale_rows(3)
+        nc.sync.dma_start(q_raw[0][:], query.rearrange("(p j) q -> p j q", j=PACK))
+        nc.sync.dma_start(q_raw[1][:], query2.rearrange("(p j) q -> p j q", j=PACK))
+        for c in range(E_TILES):
+            load_values(c)
+
+        factor_ps = psum.tile([P, P], F32, name="factor_ps")
+        nc.tensor.transpose(factor_ps[:], factor_rows[:], ident[:])
+        factors = held.tile([P, 2 * PACK], F32, name="factors")
+        nc.scalar.copy(factors[:], factor_ps[:, 0 : 2 * PACK])
+        os_by_place = factors[:, 0:PACK].unsqueeze(1).to_broadcast([P, P, PACK])
+        vsc_by_place = factors[:, PACK : 2 * PACK].unsqueeze(1).to_broadcast([P, P, PACK])
+
+        key_codes = held.tile([P, SLOTS], U32, name="key_codes", align_bytes=64)
+        key_scale = held.tile([P, SLOTS], U8, name="key_scale", align_bytes=64)
+        nc.vector.tensor_copy(dealt(key_codes[:]), key_words[:].bitcast(U32).indirect(idx[:]))
+        nc.vector.tensor_copy(dealt(key_scale[:]), key_bytes[:].indirect(idx[:]))
+
+        q_bf = held.tile([P, 2, Q, PACK], BF16, name="q_bf", align_bytes=64)
+        for n in range(2):
+            nc.vector.tensor_copy(q_bf[:, n, :, :], q_raw[n][:].rearrange("p j q -> p q j"))
+        q_codes = held.tile([P, 2 * Q], U32, name="q_codes", align_bytes=64)
+        q_scale = held.tile([P, 2 * Q], U8, name="q_scale", align_bytes=64)
+        nc.vector.quantize_mx(q_codes[:].bitcast(FP8X4), q_scale[:], q_bf[:].rearrange("p n q j -> p (n q j)"))
+
+        note_got = held.tile([P, PACK, SLOTS], F32, name="note_got")
+        for j in range(PACK):
+            nc.scalar.activation(note_got[:, j, :], note_pair[j // 2][:, j % 2, :].indirect(idx2[:]), COPY)
+        note_woven = held.tile([P, SLOTS * PACK], BF16, name="note_woven", align_bytes=64)
+        nc.vector.tensor_copy(
+            note_woven[:].rearrange("p (t b r j) -> p t b r j", t=PACK, b=BLOCKS, r=RUN),
+            note_got[:].rearrange("p j (b t r) -> p t b r j", t=PACK, r=RUN),
+        )
+        note_codes = held.tile([P, SLOTS], U32, name="note_codes", align_bytes=64)
+        note_scale = held.tile([P, SLOTS], U8, name="note_scale", align_bytes=64)
+        nc.vector.quantize_mx(note_codes[:].bitcast(FP8X4), note_scale[:], note_woven[:])
+
+        w_ps = psum.tile([P, PACK, Q], F32, name="w_ps")
+        for t in range(PACK):
+            cols = slice(t * P, (t + 1) * P)
+            for n, (codes, scale) in enumerate(((key_codes, key_scale), (note_codes, note_scale))):
+                qcols = slice(n * Q, (n + 1) * Q)
+                nc.tensor.matmul_mx(
+                    w_ps[:, t, :],
+                    lhsT=codes[:, cols].bitcast(FP8X4),
+                    lhsT_scale=scale[:, cols],
+                    rhs=q_codes[:, qcols].bitcast(FP8X4),
+                    rhs_scale=q_scale[:, qcols],
+                    start=(n == 0),
+                    stop=(n == 1),
+                )
+        w_bf = held.tile([P, Q, PACK], BF16, name="w_bf", align_bytes=64)
+        nc.vector.tensor_tensor(w_bf[:], w_ps[:].rearrange("p t q -> p q t"), os_by_place, MULT)
+        w_codes = held.tile([P, Q], U32, name="w_codes", align_bytes=64)
+        w_scale = held.tile([P, Q], U8, name="w_scale", align_bytes=64)
+        nc.vector.quantize_mx(w_codes[:].bitcast(FP8X4), w_scale[:], w_bf[:].rearrange("p q t -> p (q t)"))
+
+        for c in range(E_TILES):
+            got_a = work.tile([P, SLOTS], F32, name="got_a")
+            got_b = work.tile([P, SLOTS], F32, name="got_b")
+            nc.scalar.activation(got_a[:], val_a[c][:].indirect(idx[:]), COPY)
+            cut = 16 * VECTOR_COLS
+            nc.vector.tensor_copy(got_b[:, :cut], val_b[c][:].indirect(idx3[:, :VECTOR_COLS]))
+            nc.scalar.activation(got_b[:, cut:], val_b[c][:].indirect(idx3[:, VECTOR_COLS:]), COPY)
+            larger = work.tile([P, SLOTS], F32, name="larger")
+            nc.vector.tensor_tensor(dealt(larger[:]), listed(got_a[:]), listed(got_b[:]), MAX)
+            turned = psum2.tile([P, PACK, P], F32, name="turned")
+            for t in range(PACK):
+                nc.tensor.transpose(turned[:, t, :], larger[:, t * P : (t + 1) * P], ident[:])
+            v_bf = work.tile([P, P, PACK], BF16, name="v_bf", align_bytes=64)
+            nc.vector.tensor_tensor(v_bf[:], turned[:].rearrange("p t e -> p e t"), vsc_by_place, MULT)
+            v_codes = work.tile([P, P], U32, name="v_codes", align_bytes=64)
+            v_scale = work.tile([P, P], U8, name="v_scale", align_bytes=64)
+            nc.vector.quantize_mx(v_codes[:].bitcast(FP8X4), v_scale[:], v_bf[:].rearrange("p e t -> p (e t)"))
+            out_ps = psum2.tile([P, P], F32, name="out_ps")
+            nc.tensor.matmul_mx(
+                out_ps[:],
+                lhsT=w_codes[:].bitcast(FP8X4),
+                lhsT_scale=w_scale[:],
+                rhs=v_codes[:].bitcast(FP8X4),
+                rhs_scale=v_scale[:],
+                start=True,
+                stop=True,
+            )
+            result = held.tile([P, P], F32, name="result%d" % c, tag="val_b%d" % (c + 1))
+            nc.scalar.copy(result[:], out_ps[:])
+            nc.sync.dma_start(out[:, c * P : (c + 1) * P], result[:])

@@ -21,7 +21,7 @@ BLOCKS = SLOTS // 32
 RUN = 8
 E_TILES = E // P
 LIST_COLS = SLOTS // 16
-VECTOR_COLS = 20
+VECTOR_COLS = 18
 
 FLOPS = 2 * Q * SLOTS * D * 2 + 2 * Q * E * SLOTS
 
@@ -50,9 +50,9 @@ def tile_attend_twosources_mergedvalues_lean_kernel(
         key_words = held.tile([P, T], I32, name="key_words")
         key_bytes = held.tile([P, T], U8, name="key_bytes")
         q_raw = [held.tile([P, PACK, Q], F32, name="q_raw%d" % n) for n in range(2)]
-        note_pair = [held.tile([P, 2, U], F32, name="note_pair%d" % h) for h in range(2)]
-        val_a = [held.tile([P, T], F32, name="val_a%d" % c) for c in range(E_TILES)]
-        val_b = [held.tile([P, X], F32, name="val_b%d" % c, tag="val_b%d" % c) for c in range(E_TILES)]
+        note_plane = [held.tile([P, U], F32, name="note_plane%d" % j) for j in range(PACK)]
+        val_a = [held.tile([P, T], F32, name="val_a%d" % c, tag="val_a%d" % c) for c in range(E_TILES)]
+        val_b = [held.tile([P, X], F32, name="val_b%d" % c) for c in range(E_TILES)]
         factor_rows = held.tile([P, P], F32, name="factor_rows")
         ident = held.tile([P, P], F32, name="ident")
 
@@ -60,36 +60,27 @@ def tile_attend_twosources_mergedvalues_lean_kernel(
         nc.gpsimd.memset(factor_rows[:], 0.0)
         make_identity(nc, ident[:])
 
-        notes_by_row = notes.rearrange("(p j) u -> p j u", j=PACK)
+        notes_by_plane = notes.rearrange("(p j) u -> j p u", j=PACK)
         scale_rows = keys_scales[0].bitcast(I32)
-
-        def load_scale_rows(r):
-            nc.sync.dma_start(key_bytes[r:P:32, :].bitcast(I32), scale_rows[r:16:4, :])
-
-        def load_values(c):
-            nc.sync.dma_start(val_a[c][:], vals[c * P : (c + 1) * P, :])
-            if c == 0:
-                for n, vec in enumerate((osc, vsc)):
-                    nc.sync.dma_start(
-                        factor_rows[PACK * n : PACK * (n + 1), :].rearrange("t (b r) -> t b r", r=RUN),
-                        vec[0].rearrange("(b t r) -> t b r", t=PACK, r=RUN),
-                    )
-                nc.sync.dma_start(idx3[:], offs3)
-            nc.sync.dma_start(val_b[c][:], vals2[c * P : (c + 1) * P, :])
-
+        nc.sync.dma_start(note_plane[0][:], notes_by_plane[0])
+        nc.sync.dma_start(idx2[:], offs2)
         nc.sync.dma_start(key_words[:], keys_words[0].rearrange("p c r -> p (c r)").bitcast(I32))
         nc.sync.dma_start(idx[:], offs)
-        nc.sync.dma_start(idx2[:], offs2)
-        nc.sync.dma_start(note_pair[0][:], notes_by_row[:, 0:2, :])
-        load_scale_rows(0)
-        load_scale_rows(1)
-        nc.sync.dma_start(note_pair[1][:], notes_by_row[:, 2:4, :])
-        load_scale_rows(2)
-        load_scale_rows(3)
-        nc.sync.dma_start(q_raw[0][:], query.rearrange("(p j) q -> p j q", j=PACK))
-        nc.sync.dma_start(q_raw[1][:], query2.rearrange("(p j) q -> p j q", j=PACK))
+        for r in range(4):
+            nc.sync.dma_start(key_bytes[r:P:32, :].bitcast(I32), scale_rows[r:16:4, :])
+        for j in range(1, PACK):
+            nc.sync.dma_start(note_plane[j][:], notes_by_plane[j])
+        for n, source in enumerate((query, query2)):
+            nc.sync.dma_start(q_raw[n][:], source.rearrange("(p j) q -> p j q", j=PACK))
+        for n, vec in enumerate((osc, vsc)):
+            nc.sync.dma_start(
+                factor_rows[PACK * n : PACK * (n + 1), :].rearrange("t (b r) -> t b r", r=RUN),
+                vec[0].rearrange("(b t r) -> t b r", t=PACK, r=RUN),
+            )
+        nc.sync.dma_start(idx3[:], offs3)
         for c in range(E_TILES):
-            load_values(c)
+            nc.sync.dma_start(val_b[c][:], vals2[c * P : (c + 1) * P, :])
+            nc.sync.dma_start(val_a[c][:], vals[c * P : (c + 1) * P, :])
 
         factor_ps = psum.tile([P, P], F32, name="factor_ps")
         nc.tensor.transpose(factor_ps[:], factor_rows[:], ident[:])
@@ -105,14 +96,15 @@ def tile_attend_twosources_mergedvalues_lean_kernel(
 
         q_bf = held.tile([P, 2, Q, PACK], BF16, name="q_bf", align_bytes=64)
         for n in range(2):
-            nc.vector.tensor_copy(q_bf[:, n, :, :], q_raw[n][:].rearrange("p j q -> p q j"))
+            nc.scalar.copy(q_bf[:, n, :, :], q_raw[n][:].rearrange("p j q -> p q j"))
         q_codes = held.tile([P, 2 * Q], U32, name="q_codes", align_bytes=64)
         q_scale = held.tile([P, 2 * Q], U8, name="q_scale", align_bytes=64)
         nc.vector.quantize_mx(q_codes[:].bitcast(FP8X4), q_scale[:], q_bf[:].rearrange("p n q j -> p (n q j)"))
 
-        note_got = held.tile([P, PACK, SLOTS], F32, name="note_got")
-        for j in range(PACK):
-            nc.scalar.activation(note_got[:, j, :], note_pair[j // 2][:, j % 2, :].indirect(idx2[:]), COPY)
+        note_got = held.tile([P, PACK, SLOTS], BF16, name="note_got")
+        for j in range(PACK - 1):
+            nc.scalar.activation(note_got[:, j, :], note_plane[j][:].indirect(idx2[:]), COPY)
+        nc.vector.tensor_copy(note_got[:, PACK - 1, :], note_plane[PACK - 1][:].indirect(idx2[:]))
         note_woven = held.tile([P, SLOTS * PACK], BF16, name="note_woven", align_bytes=64)
         nc.vector.tensor_copy(
             note_woven[:].rearrange("p (t b r j) -> p t b r j", t=PACK, b=BLOCKS, r=RUN),
@@ -136,29 +128,33 @@ def tile_attend_twosources_mergedvalues_lean_kernel(
                     start=(n == 0),
                     stop=(n == 1),
                 )
-        w_bf = held.tile([P, Q, PACK], BF16, name="w_bf", align_bytes=64)
-        nc.vector.tensor_tensor(w_bf[:], w_ps[:].rearrange("p t q -> p q t"), os_by_place, MULT)
-        w_codes = held.tile([P, Q], U32, name="w_codes", align_bytes=64)
-        w_scale = held.tile([P, Q], U8, name="w_scale", align_bytes=64)
-        nc.vector.quantize_mx(w_codes[:].bitcast(FP8X4), w_scale[:], w_bf[:].rearrange("p q t -> p (q t)"))
 
-        for c in range(E_TILES):
-            got_a = work.tile([P, SLOTS], F32, name="got_a")
+        def scale_and_quantise(bank, by_place, codes, scale):
+            woven = held.tile([P, P, PACK], BF16, name="woven", tag="turns", align_bytes=64)
+            nc.vector.tensor_tensor(woven[:], bank[:].rearrange("p t x -> p x t"), by_place, MULT)
+            nc.vector.quantize_mx(codes[:].bitcast(FP8X4), scale[:], woven[:].rearrange("p x t -> p (x t)"))
+
+        def gather_and_turn(c):
             got_b = work.tile([P, SLOTS], F32, name="got_b")
-            nc.scalar.activation(got_a[:], val_a[c][:].indirect(idx[:]), COPY)
+            nc.scalar.activation(got_b[:], val_b[c][:].indirect(idx3[:]), COPY)
+            got_a = held.tile([P, SLOTS], F32, name="got_a", tag="turns", align_bytes=64)
             cut = 16 * VECTOR_COLS
-            nc.vector.tensor_copy(got_b[:, :cut], val_b[c][:].indirect(idx3[:, :VECTOR_COLS]))
-            nc.scalar.activation(got_b[:, cut:], val_b[c][:].indirect(idx3[:, VECTOR_COLS:]), COPY)
+            nc.vector.tensor_copy(got_a[:, :cut], val_a[c][:].indirect(idx[:, :VECTOR_COLS]))
+            nc.scalar.activation(got_a[:, cut:], val_a[c][:].indirect(idx[:, VECTOR_COLS:]), COPY)
             larger = work.tile([P, SLOTS], F32, name="larger")
             nc.vector.tensor_tensor(dealt(larger[:]), listed(got_a[:]), listed(got_b[:]), MAX)
             turned = psum2.tile([P, PACK, P], F32, name="turned")
             for t in range(PACK):
                 nc.tensor.transpose(turned[:, t, :], larger[:, t * P : (t + 1) * P], ident[:])
-            v_bf = work.tile([P, P, PACK], BF16, name="v_bf", align_bytes=64)
-            nc.vector.tensor_tensor(v_bf[:], turned[:].rearrange("p t e -> p e t"), vsc_by_place, MULT)
+            return turned
+
+        w_codes = held.tile([P, Q], U32, name="w_codes", align_bytes=64)
+        w_scale = held.tile([P, Q], U8, name="w_scale", align_bytes=64)
+
+        def multiply_and_store(c, turned):
             v_codes = work.tile([P, P], U32, name="v_codes", align_bytes=64)
             v_scale = work.tile([P, P], U8, name="v_scale", align_bytes=64)
-            nc.vector.quantize_mx(v_codes[:].bitcast(FP8X4), v_scale[:], v_bf[:].rearrange("p e t -> p (e t)"))
+            scale_and_quantise(turned, vsc_by_place, v_codes, v_scale)
             out_ps = psum2.tile([P, P], F32, name="out_ps")
             nc.tensor.matmul_mx(
                 out_ps[:],
@@ -169,6 +165,13 @@ def tile_attend_twosources_mergedvalues_lean_kernel(
                 start=True,
                 stop=True,
             )
-            result = held.tile([P, P], F32, name="result%d" % c, tag="val_b%d" % (c + 1))
+            result = held.tile([P, P], F32, name="result%d" % c, tag="val_a%d" % (c + 2))
             nc.scalar.copy(result[:], out_ps[:])
             nc.sync.dma_start(out[:, c * P : (c + 1) * P], result[:])
+
+        turned = [gather_and_turn(0)]
+        scale_and_quantise(w_ps, os_by_place, w_codes, w_scale)
+        for c in range(1, E_TILES):
+            turned.append(gather_and_turn(c))
+            multiply_and_store(c - 1, turned[c - 1])
+        multiply_and_store(E_TILES - 1, turned[E_TILES - 1])

@@ -50,7 +50,7 @@ def tile_attend_twosources_mergedvalues_lean_kernel(
         key_words = held.tile([P, T], I32, name="key_words")
         key_bytes = held.tile([P, T], U8, name="key_bytes")
         q_raw = [held.tile([P, PACK, Q], F32, name="q_raw%d" % n) for n in range(2)]
-        note_plane = [held.tile([P, U], F32, name="note_plane%d" % j) for j in range(PACK)]
+        note_pair = [held.tile([P, 2, U], F32, name="note_pair%d" % h) for h in range(2)]
         val_a = [held.tile([P, T], F32, name="val_a%d" % c, tag="val_a%d" % c) for c in range(E_TILES)]
         val_b = [held.tile([P, X], F32, name="val_b%d" % c) for c in range(E_TILES)]
         factor_rows = held.tile([P, P], F32, name="factor_rows")
@@ -60,23 +60,22 @@ def tile_attend_twosources_mergedvalues_lean_kernel(
         nc.gpsimd.memset(factor_rows[:], 0.0)
         make_identity(nc, ident[:])
 
-        notes_by_plane = notes.rearrange("(p j) u -> j p u", j=PACK)
+        notes_by_row = notes.rearrange("(p j) u -> p j u", j=PACK)
         scale_rows = keys_scales[0].bitcast(I32)
-        nc.sync.dma_start(note_plane[0][:], notes_by_plane[0])
+        nc.sync.dma_start(note_pair[0][:], notes_by_row[:, 0:2, :])
         nc.sync.dma_start(idx2[:], offs2)
-        nc.sync.dma_start(key_words[:], keys_words[0].rearrange("p c r -> p (c r)").bitcast(I32))
         nc.sync.dma_start(idx[:], offs)
         for r in range(4):
             nc.sync.dma_start(key_bytes[r:P:32, :].bitcast(I32), scale_rows[r:16:4, :])
-        for j in range(1, PACK):
-            nc.sync.dma_start(note_plane[j][:], notes_by_plane[j])
-        for n, source in enumerate((query, query2)):
-            nc.sync.dma_start(q_raw[n][:], source.rearrange("(p j) q -> p j q", j=PACK))
+        nc.sync.dma_start(note_pair[1][:], notes_by_row[:, 2:4, :])
         for n, vec in enumerate((osc, vsc)):
             nc.sync.dma_start(
                 factor_rows[PACK * n : PACK * (n + 1), :].rearrange("t (b r) -> t b r", r=RUN),
                 vec[0].rearrange("(b t r) -> t b r", t=PACK, r=RUN),
             )
+        nc.sync.dma_start(key_words[:], keys_words[0].rearrange("p c r -> p (c r)").bitcast(I32))
+        for n, source in enumerate((query, query2)):
+            nc.sync.dma_start(q_raw[n][:], source.rearrange("(p j) q -> p j q", j=PACK))
         nc.sync.dma_start(idx3[:], offs3)
         for c in range(E_TILES):
             nc.sync.dma_start(val_b[c][:], vals2[c * P : (c + 1) * P, :])
@@ -91,7 +90,6 @@ def tile_attend_twosources_mergedvalues_lean_kernel(
 
         key_codes = held.tile([P, SLOTS], U32, name="key_codes", align_bytes=64)
         key_scale = held.tile([P, SLOTS], U8, name="key_scale", align_bytes=64)
-        nc.vector.tensor_copy(dealt(key_codes[:]), key_words[:].bitcast(U32).indirect(idx[:]))
         nc.vector.tensor_copy(dealt(key_scale[:]), key_bytes[:].indirect(idx[:]))
 
         q_bf = held.tile([P, 2, Q, PACK], BF16, name="q_bf", align_bytes=64)
@@ -101,10 +99,10 @@ def tile_attend_twosources_mergedvalues_lean_kernel(
         q_scale = held.tile([P, 2 * Q], U8, name="q_scale", align_bytes=64)
         nc.vector.quantize_mx(q_codes[:].bitcast(FP8X4), q_scale[:], q_bf[:].rearrange("p n q j -> p (n q j)"))
 
-        note_got = held.tile([P, PACK, SLOTS], BF16, name="note_got")
-        for j in range(PACK - 1):
-            nc.scalar.activation(note_got[:, j, :], note_plane[j][:].indirect(idx2[:]), COPY)
-        nc.vector.tensor_copy(note_got[:, PACK - 1, :], note_plane[PACK - 1][:].indirect(idx2[:]))
+        note_got = held.tile([P, PACK, SLOTS], F32, name="note_got")
+        for h in range(2):
+            nc.scalar.activation(note_got[:, 2 * h, :], note_pair[h][:, 0, :].indirect(idx2[:]), COPY)
+            nc.vector.tensor_copy(note_got[:, 2 * h + 1, :], note_pair[h][:, 1, :].indirect(idx2[:]))
         note_woven = held.tile([P, SLOTS * PACK], BF16, name="note_woven", align_bytes=64)
         nc.vector.tensor_copy(
             note_woven[:].rearrange("p (t b r j) -> p t b r j", t=PACK, b=BLOCKS, r=RUN),
@@ -113,6 +111,8 @@ def tile_attend_twosources_mergedvalues_lean_kernel(
         note_codes = held.tile([P, SLOTS], U32, name="note_codes", align_bytes=64)
         note_scale = held.tile([P, SLOTS], U8, name="note_scale", align_bytes=64)
         nc.vector.quantize_mx(note_codes[:].bitcast(FP8X4), note_scale[:], note_woven[:])
+
+        nc.vector.tensor_copy(dealt(key_codes[:]), key_words[:].bitcast(U32).indirect(idx[:]))
 
         w_ps = psum.tile([P, PACK, Q], F32, name="w_ps")
         for t in range(PACK):
@@ -129,32 +129,38 @@ def tile_attend_twosources_mergedvalues_lean_kernel(
                     stop=(n == 1),
                 )
 
-        def scale_and_quantise(bank, by_place, codes, scale):
-            woven = held.tile([P, P, PACK], BF16, name="woven", tag="turns", align_bytes=64)
+        def scale_and_weave(woven, bank, by_place):
             nc.vector.tensor_tensor(woven[:], bank[:].rearrange("p t x -> p x t"), by_place, MULT)
-            nc.vector.quantize_mx(codes[:].bitcast(FP8X4), scale[:], woven[:].rearrange("p x t -> p (x t)"))
-
-        def gather_and_turn(c):
-            got_b = work.tile([P, SLOTS], F32, name="got_b")
-            nc.scalar.activation(got_b[:], val_b[c][:].indirect(idx3[:]), COPY)
-            got_a = held.tile([P, SLOTS], F32, name="got_a", tag="turns", align_bytes=64)
-            cut = 16 * VECTOR_COLS
-            nc.vector.tensor_copy(got_a[:, :cut], val_a[c][:].indirect(idx[:, :VECTOR_COLS]))
-            nc.scalar.activation(got_a[:, cut:], val_a[c][:].indirect(idx[:, VECTOR_COLS:]), COPY)
-            larger = work.tile([P, SLOTS], F32, name="larger")
-            nc.vector.tensor_tensor(dealt(larger[:]), listed(got_a[:]), listed(got_b[:]), MAX)
-            turned = psum2.tile([P, PACK, P], F32, name="turned")
-            for t in range(PACK):
-                nc.tensor.transpose(turned[:, t, :], larger[:, t * P : (t + 1) * P], ident[:])
-            return turned
+            return woven[:].rearrange("p x t -> p (x t)")
 
         w_codes = held.tile([P, Q], U32, name="w_codes", align_bytes=64)
         w_scale = held.tile([P, Q], U8, name="w_scale", align_bytes=64)
 
-        def multiply_and_store(c, turned):
-            v_codes = work.tile([P, P], U32, name="v_codes", align_bytes=64)
+        def gather_and_turn(c):
+            got_b = work.tile([P, SLOTS], F32, name="got_b")
+            nc.scalar.activation(got_b[:], val_b[c][:].indirect(idx3[:]), COPY)
+            got_a = held.tile([P, SLOTS], F32, name="got_a", tag="turn%d" % (c % 2), align_bytes=64)
+            cut = 16 * VECTOR_COLS
+            nc.vector.tensor_copy(got_a[:, :cut], val_a[c][:].indirect(idx[:, :VECTOR_COLS]))
+            nc.scalar.activation(got_a[:, cut:], val_a[c][:].indirect(idx[:, VECTOR_COLS:]), COPY)
+            larger = work.tile([P, SLOTS], F32, name="larger")
+            turned = psum2.tile([P, PACK, P], F32, name="turned")
+            for first in range(0, PACK, 2):
+                places = slice(first, first + 2)
+                nc.vector.tensor_tensor(
+                    dealt(larger[:])[:, :, places, :],
+                    listed(got_a[:])[:, :, places, :],
+                    listed(got_b[:])[:, :, places, :],
+                    MAX,
+                )
+                for t in range(first, first + 2):
+                    nc.tensor.transpose(turned[:, t, :], larger[:, t * P : (t + 1) * P], ident[:])
+            return turned
+
+        def multiply_and_store(c, woven):
+            v_codes = held.tile([P, P], U32, name="v_codes", tag="turn%d" % ((c + 1) % 2), align_bytes=64)
             v_scale = work.tile([P, P], U8, name="v_scale", align_bytes=64)
-            scale_and_quantise(turned, vsc_by_place, v_codes, v_scale)
+            nc.vector.quantize_mx(v_codes[:].bitcast(FP8X4), v_scale[:], woven)
             out_ps = psum2.tile([P, P], F32, name="out_ps")
             nc.tensor.matmul_mx(
                 out_ps[:],
@@ -169,9 +175,16 @@ def tile_attend_twosources_mergedvalues_lean_kernel(
             nc.scalar.copy(result[:], out_ps[:])
             nc.sync.dma_start(out[:, c * P : (c + 1) * P], result[:])
 
-        turned = [gather_and_turn(0)]
-        scale_and_quantise(w_ps, os_by_place, w_codes, w_scale)
-        for c in range(1, E_TILES):
-            turned.append(gather_and_turn(c))
-            multiply_and_store(c - 1, turned[c - 1])
-        multiply_and_store(E_TILES - 1, turned[E_TILES - 1])
+        woven = []
+        for c in range(E_TILES):
+            turned = gather_and_turn(c)
+            if c == 0:
+                w_woven = held.tile([P, P, PACK], BF16, name="w_woven", tag="turn0", align_bytes=64)
+                nc.vector.quantize_mx(
+                    w_codes[:].bitcast(FP8X4), w_scale[:], scale_and_weave(w_woven, w_ps, os_by_place)
+                )
+            else:
+                multiply_and_store(c - 1, woven[c - 1])
+            v_woven = work.tile([P, P, PACK], BF16, name="v_woven", align_bytes=64)
+            woven.append(scale_and_weave(v_woven, turned, vsc_by_place))
+        multiply_and_store(E_TILES - 1, woven[E_TILES - 1])

from contextlib import ExitStack

import concourse.mybir as mybir
from concourse.masks import make_identity

F32 = mybir.dt.float32
BF16 = mybir.dt.bfloat16
I32 = mybir.dt.int32
U32 = mybir.dt.uint32
U16 = mybir.dt.uint16
U8 = mybir.dt.uint8
FP8X4 = mybir.dt.float8_e4m3fn_x4
COPY = mybir.ActivationFunctionType.Copy
MULT = mybir.AluOpType.mult
MAX = mybir.AluOpType.max

P = 128
PACK = 4
D, T, SLOTS, Q, E, U, X = 512, 2048, 512, 128, 512, 1024, 1024
BLOCKS = SLOTS // 32
RUN = 8
E_TILES = E // P
LIST_COLS = SLOTS // 16
VECTOR_COLS = 18

FLOPS = 2 * Q * SLOTS * D * 2 + 2 * Q * E * SLOTS


def dealt(ap):
    return ap.rearrange("p (t b r) -> p b t r", t=PACK, b=BLOCKS, r=RUN)


def listed(ap):
    return ap.rearrange("p (b t r) -> p b t r", t=PACK, b=BLOCKS, r=RUN)


def tile_attend_twosources_mergedvalues_lean_kernel(
    tc, query, query2, keys_words, keys_scales, notes, osc, vals, vals2, vsc, offs, offs2, offs3, out
):
    nc = tc.nc
    with ExitStack() as ctx:
        held = ctx.enter_context(tc.tile_pool(name="held", bufs=1))
        work = ctx.enter_context(tc.tile_pool(name="work", bufs=2))
        psum = ctx.enter_context(tc.psum_pool(name="psum", bufs=1))
        psum2 = ctx.enter_context(tc.psum_pool(name="psum2", bufs=2))

        idx = held.tile([P, LIST_COLS], U16, name="idx")
        idx2 = held.tile([P, LIST_COLS], U16, name="idx2")
        idx3 = held.tile([P, LIST_COLS], U16, name="idx3")
        key_words = held.tile([P, T], I32, name="key_words")
        key_bytes = held.tile([P, T], U8, name="key_bytes")
        q_raw = [held.tile([P, PACK, Q], F32, name="q_raw%d" % n) for n in range(2)]
        note_pair = [held.tile([P, 2, U], F32, name="note_pair%d" % h) for h in range(2)]
        val_a = [held.tile([P, T], F32, name="val_a%d" % c, tag="val_a%d" % c) for c in range(E_TILES)]
        val_b = [held.tile([P, X], F32, name="val_b%d" % c) for c in range(E_TILES)]
        factor_rows = held.tile([P, P], F32, name="factor_rows")
        ident = held.tile([P, P], F32, name="ident")

        nc.gpsimd.memset(key_bytes[:].bitcast(I32), 0)
        nc.gpsimd.memset(factor_rows[:], 0.0)
        make_identity(nc, ident[:])

        notes_by_row = notes.rearrange("(p j) u -> p j u", j=PACK)
        scale_rows = keys_scales[0].bitcast(I32)
        nc.sync.dma_start(note_pair[0][:], notes_by_row[:, 0:2, :])
        nc.sync.dma_start(idx2[:], offs2)
        nc.sync.dma_start(idx[:], offs)
        for r in range(4):
            nc.sync.dma_start(key_bytes[r:P:32, :].bitcast(I32), scale_rows[r:16:4, :])
        nc.sync.dma_start(note_pair[1][:], notes_by_row[:, 2:4, :])
        for n, vec in enumerate((osc, vsc)):
            nc.sync.dma_start(
                factor_rows[PACK * n : PACK * (n + 1), :].rearrange("t (b r) -> t b r", r=RUN),
                vec[0].rearrange("(b t r) -> t b r", t=PACK, r=RUN),
            )
        nc.sync.dma_start(key_words[:], keys_words[0].rearrange("p c r -> p (c r)").bitcast(I32))
        for n, source in enumerate((query, query2)):
            nc.sync.dma_start(q_raw[n][:], source.rearrange("(p j) q -> p j q", j=PACK))
        nc.sync.dma_start(idx3[:], offs3)
        for c in range(E_TILES):
            nc.sync.dma_start(val_b[c][:], vals2[c * P : (c + 1) * P, :])
            nc.sync.dma_start(val_a[c][:], vals[c * P : (c + 1) * P, :])

        factor_ps = psum.tile([P, P], F32, name="factor_ps")
        nc.tensor.transpose(factor_ps[:], factor_rows[:], ident[:])
        factors = held.tile([P, 2 * PACK], F32, name="factors")
        nc.scalar.copy(factors[:], factor_ps[:, 0 : 2 * PACK])
        os_by_place = factors[:, 0:PACK].unsqueeze(1).to_broadcast([P, P, PACK])
        vsc_by_place = factors[:, PACK : 2 * PACK].unsqueeze(1).to_broadcast([P, P, PACK])

        key_codes = held.tile([P, SLOTS], U32, name="key_codes", align_bytes=64)
        key_scale = held.tile([P, SLOTS], U8, name="key_scale", align_bytes=64)
        nc.vector.tensor_copy(dealt(key_scale[:]), key_bytes[:].indirect(idx[:]))

        q_bf = held.tile([P, 2, Q, PACK], BF16, name="q_bf", align_bytes=64)
        for n in range(2):
            nc.scalar.copy(q_bf[:, n, :, :], q_raw[n][:].rearrange("p j q -> p q j"))
        q_codes = held.tile([P, 2 * Q], U32, name="q_codes", align_bytes=64)
        q_scale = held.tile([P, 2 * Q], U8, name="q_scale", align_bytes=64)
        nc.vector.quantize_mx(q_codes[:].bitcast(FP8X4), q_scale[:], q_bf[:].rearrange("p n q j -> p (n q j)"))

        note_got = held.tile([P, PACK, SLOTS], F32, name="note_got")
        for h in range(2):
            nc.scalar.activation(note_got[:, 2 * h, :], note_pair[h][:, 0, :].indirect(idx2[:]), COPY)
            nc.vector.tensor_copy(note_got[:, 2 * h + 1, :], note_pair[h][:, 1, :].indirect(idx2[:]))
        note_woven = held.tile([P, SLOTS * PACK], BF16, name="note_woven", align_bytes=64)
        nc.vector.tensor_copy(
            note_woven[:].rearrange("p (t b r j) -> p t b r j", t=PACK, b=BLOCKS, r=RUN),
            note_got[:].rearrange("p j (b t r) -> p t b r j", t=PACK, r=RUN),
        )
        note_codes = held.tile([P, SLOTS], U32, name="note_codes", align_bytes=64)
        note_scale = held.tile([P, SLOTS], U8, name="note_scale", align_bytes=64)
        nc.vector.quantize_mx(note_codes[:].bitcast(FP8X4), note_scale[:], note_woven[:])

        nc.vector.tensor_copy(dealt(key_codes[:]), key_words[:].bitcast(U32).indirect(idx[:]))

        w_ps = psum.tile([P, PACK, Q], F32, name="w_ps")
        for t in range(PACK):
            cols = slice(t * P, (t + 1) * P)
            for n, (codes, scale) in enumerate(((key_codes, key_scale), (note_codes, note_scale))):
                qcols = slice(n * Q, (n + 1) * Q)
                nc.tensor.matmul_mx(
                    w_ps[:, t, :],
                    lhsT=codes[:, cols].bitcast(FP8X4),
                    lhsT_scale=scale[:, cols],
                    rhs=q_codes[:, qcols].bitcast(FP8X4),
                    rhs_scale=q_scale[:, qcols],
                    start=(n == 0),
                    stop=(n == 1),
                )

        def scale_and_weave(woven, bank, by_place):
            nc.vector.tensor_tensor(woven[:], bank[:].rearrange("p t x -> p x t"), by_place, MULT)
            return woven[:].rearrange("p x t -> p (x t)")

        w_codes = held.tile([P, Q], U32, name="w_codes", align_bytes=64)
        w_scale = held.tile([P, Q], U8, name="w_scale", align_bytes=64)

        def gather_and_turn(c):
            got_b = work.tile([P, SLOTS], F32, name="got_b")
            nc.scalar.activation(got_b[:], val_b[c][:].indirect(idx3[:]), COPY)
            got_a = held.tile([P, SLOTS], F32, name="got_a", tag="turn%d" % (c % 2), align_bytes=64)
            cut = 16 * VECTOR_COLS
            nc.vector.tensor_copy(got_a[:, :cut], val_a[c][:].indirect(idx[:, :VECTOR_COLS]))
            nc.scalar.activation(got_a[:, cut:], val_a[c][:].indirect(idx[:, VECTOR_COLS:]), COPY)
            larger = work.tile([P, SLOTS], F32, name="larger")
            turned = psum2.tile([P, PACK, P], F32, name="turned")
            for first in range(0, PACK, 2):
                places = slice(first, first + 2)
                nc.vector.tensor_tensor(
                    dealt(larger[:])[:, :, places, :],
                    listed(got_a[:])[:, :, places, :],
                    listed(got_b[:])[:, :, places, :],
                    MAX,
                )
                for t in range(first, first + 2):
                    nc.tensor.transpose(turned[:, t, :], larger[:, t * P : (t + 1) * P], ident[:])
            return turned

        def multiply_and_store(c, woven):
            v_codes = held.tile([P, P], U32, name="v_codes", tag="turn%d" % ((c + 1) % 2), align_bytes=64)
            v_scale = work.tile([P, P], U8, name="v_scale", align_bytes=64)
            nc.vector.quantize_mx(v_codes[:].bitcast(FP8X4), v_scale[:], woven)
            out_ps = psum2.tile([P, P], F32, name="out_ps")
            nc.tensor.matmul_mx(
                out_ps[:],
                lhsT=w_codes[:].bitcast(FP8X4),
                lhsT_scale=w_scale[:],
                rhs=v_codes[:].bitcast(FP8X4),
                rhs_scale=v_scale[:],
                start=True,
                stop=True,
            )
            result = held.tile([P, P], F32, name="result%d" % c, tag="val_a%d" % (c + 2))
            nc.scalar.copy(result[:], out_ps[:])
            nc.sync.dma_start(out[:, c * P : (c + 1) * P], result[:])

        woven = []
        for c in range(E_TILES):
            turned = gather_and_turn(c)
            if c == 0:
                w_woven = held.tile([P, P, PACK], BF16, name="w_woven", tag="turn0", align_bytes=64)
                nc.vector.quantize_mx(
                    w_codes[:].bitcast(FP8X4), w_scale[:], scale_and_weave(w_woven, w_ps, os_by_place)
                )
            else:
                multiply_and_store(c - 1, woven[c - 1])
            v_woven = work.tile([P, P, PACK], BF16, name="v_woven", align_bytes=64)
            woven.append(scale_and_weave(v_woven, turned, vsc_by_place))
        multiply_and_store(E_TILES - 1, woven[E_TILES - 1])
